import numpy as np
import ml_dtypes


def mxq(x, axis, fmt="e4m3"):
    dtype, down = {"e4m3": (ml_dtypes.float8_e4m3fn, 7), "e5m2": (ml_dtypes.float8_e5m2, 14)}[fmt]
    v = np.moveaxis(np.asarray(x, np.float32).astype(ml_dtypes.bfloat16).astype(np.float64), axis, -1)
    blocks = v.reshape(v.shape[:-1] + (-1, 32))
    amax = np.abs(blocks).max(-1, keepdims=True)
    byte = np.maximum(np.where(amax > 0, np.frexp(amax)[1] - 1 + 127, 0) - down, 1)
    scale = np.exp2(byte - 127.0)
    codes = (blocks / scale).astype(np.float32).astype(dtype).astype(np.float64)
    return np.moveaxis((codes * scale).reshape(v.shape), -1, axis)


WIDE = False


def mx_kscale(k):
    if not WIDE:
        return np.ones(k)
    levels = np.array([10, -10, 5, -5, 0])
    if k % 512:
        return np.exp2(np.random.permutation(np.resize(levels, k // 32))).repeat(32)
    a = np.empty((k // 512, 16))
    for p in range(k // 512):
        a[p, :8] = np.random.permutation(np.resize(levels, 8))
        for g in range(8):
            far = levels[np.abs(levels - a[p, g]) >= 10]
            a[p, g + 8] = far[np.random.randint(len(far))]
    return np.exp2(a.ravel()).repeat(32)


def f64(x):
    return np.asarray(x).astype(np.float64)


def striped(idx):
    return np.tile(idx.reshape(-1, 16).T, (8, 1)).astype(np.uint16)


def unstriped(offs):
    return offs[:16].T.reshape(-1).astype(np.int64)


def striped8(idx):
    return np.concatenate([x.reshape(-1, 16).T for x in idx]).astype(np.uint16)


def runs(offs, k):
    lists = np.stack([offs[16 * r : 16 * r + 16].T.reshape(-1) for r in range(8)]).astype(np.int64)
    return lists[np.arange(k) % 512 // 64]


def pack_weight(w):
    k, n = w.shape
    w = f64(np.asarray(w, np.float32).astype(ml_dtypes.bfloat16)).reshape(k // 32, 32, n)
    amax = np.abs(w).max(1)
    byte = np.clip(np.where(amax > 0, np.frexp(amax)[1] - 1 + 127 - 7, 1), 1, 254)
    scaled = (w * np.exp2(127.0 - byte)[:, None, :]).reshape(k, n).astype(np.float32)
    words = np.ascontiguousarray(scaled.reshape(k // 512, 128, 4, n).transpose(0, 1, 3, 2)).astype(ml_dtypes.float8_e4m3fn).view(np.uint8)
    return words, np.ascontiguousarray(byte.astype(np.uint8).reshape(k // 512, 16, n))


def unpack_weight(words, scales):
    g, p, n, _ = words.shape
    vals = np.ascontiguousarray(words).view(ml_dtypes.float8_e4m3fn).astype(np.float64) * np.repeat(np.exp2(scales.astype(np.float64) - 127.0), 8, axis=1)[..., None]
    return vals.transpose(0, 1, 3, 2).reshape(g * 512, n)


K, T, S, N, H = 512, 2048, 512, 512, 512


def setup_inputs():
    n = np.random.standard_normal
    s = mx_kscale(K)[:, None]
    u = mx_kscale(S)
    packed_xT = pack_weight(n((K, T)) * s)
    return {
        "x_words": packed_xT[0],
        "x_scales": packed_xT[1],
        "wa": (n((K, H)) / np.sqrt(K) / s).astype(np.float32),
        "wb": (n((K, H)) / np.sqrt(K) / s).astype(np.float32),
        "gt": (np.random.uniform(0.5, 1.5, (S, 1)) * u[:, None]).astype(np.float32),
        "w1": (n((S, N)) / np.sqrt(S) / u[:, None]).astype(np.float32),
        "offs": striped(np.random.permutation(T)[:S]),
        "two": striped(np.random.permutation(T)[:S]),
        "n1": striped(np.random.permutation(H)),
        "n2": striped(np.random.permutation(H)),
        "n3": striped8(np.stack([np.random.permutation(H) for _ in range(8)])),
        "n4": striped8(np.stack([np.random.permutation(H) for _ in range(8)])),
    }


def reference(x_words, x_scales, wa, wb, gt, w1, offs, two, n1, n2, n3, n4):
    xq = unpack_weight(x_words, x_scales)[:, unstriped(offs)]
    y = xq.T @ mxq(f64(wa), 0, "e4m3")
    x_two = unpack_weight(x_words, x_scales)[:, unstriped(two)]
    d = x_two.T @ mxq(f64(wb), 0, "e4m3")
    z = f64(gt) * (0.75 * (y * d[:, unstriped(n2)] - (y[:, unstriped(n1)] * d)))
    h = mxq(f64(w1), 0, "e4m3").T @ mxq(z, 0, "e4m3")
    return (h * (h[np.arange(N)[:, None], runs(n3, N)])) * (np.tanh(h[np.arange(N)[:, None], runs(n4, N)]))

@@ -1,0 +1,225 @@
+from contextlib import ExitStack
+
+import concourse.mybir as mybir
+
+K, T, S, N, H = 512, 2048, 512, 512, 512
+FLOPS = 2 * K * S * H * 2 + 2 * S * N * H
+
+F32 = mybir.dt.float32
+BF16 = mybir.dt.bfloat16
+I32 = mybir.dt.int32
+U32 = mybir.dt.uint32
+U16 = mybir.dt.uint16
+U8 = mybir.dt.uint8
+FP8X4 = mybir.dt.float8_e4m3fn_x4
+MULT = mybir.AluOpType.mult
+ADD = mybir.AluOpType.add
+SUB = mybir.AluOpType.subtract
+COPY = mybir.ActivationFunctionType.Copy
+TANH = mybir.ActivationFunctionType.Tanh
+
+P = 128
+PACK = 4
+HALF = 256
+SPARE = 16
+
+
+def tile_picked_twtcrossbcube_none_p_kernel(
+    tc, x_words, x_scales, wa, wb, gt, w1, offs, two, n1, n2, n3, n4, out
+):
+    nc = tc.nc
+    with ExitStack() as ctx:
+        keep = ctx.enter_context(tc.tile_pool(name="keep", bufs=1))
+        psum = ctx.enter_context(tc.psum_pool(name="psum", bufs=1))
+
+        def load_list(name, src):
+            tile = keep.tile([P, S // 16], U16, name=name)
+            nc.sync.dma_start(tile[:], src)
+            return tile
+
+        def load_half(name, w, half):
+            raw = keep.tile([P, PACK, HALF], F32, name=name)
+            cols = slice(half * HALF, (half + 1) * HALF)
+            nc.sync.dma_start(raw[:], w.rearrange("(p j) c -> p j c", j=PACK)[:, :, cols])
+            return raw
+
+        def mx_tiles(name, width):
+            grouped = keep.tile([P, width * PACK], BF16, name=name + "_bf", align_bytes=64)
+            codes = keep.tile([P, width], U32, name=name + "_codes", align_bytes=64)
+            scales = keep.tile([P, width], U8, name=name + "_scales", align_bytes=64)
+            return grouped, codes, scales
+
+        def quantize(mx):
+            grouped, codes, scales = mx
+            nc.vector.quantize_mx(out=codes[:].bitcast(FP8X4), scales=scales[:], in_=grouped[:])
+
+        def interleave(copy, mx, raw):
+            copy(
+                mx[0][:].rearrange("p (c i j) -> p c j i", i=4, j=PACK),
+                raw[:].rearrange("p j (c i) -> p c j i", i=4),
+            )
+
+        byte_table = keep.tile([P, T], U8, name="byte_table", align_bytes=64)
+        nc.vector.memset(byte_table[:].bitcast(I32), 0)
+        offs_t = load_list("offs_t", offs)
+        for q in range(4):
+            nc.sync.dma_start(
+                byte_table[32 * q : 32 * q + 4, :].bitcast(I32),
+                x_scales[0, 4 * q : 4 * q + 4, :].bitcast(I32),
+            )
+        two_t = load_list("two_t", two)
+        word_table = keep.tile([P, T], U32, name="word_table", align_bytes=64)
+        nc.sync.dma_start(
+            word_table[:].bitcast(I32), x_words[0].rearrange("p c r -> p (c r)").bitcast(I32)
+        )
+        wa_raw = [load_half("wa_raw0", wa, 0)]
+        gt_raw = keep.tile([P, PACK], F32, name="gt_raw")
+        nc.sync.dma_start(gt_raw[:], gt.rearrange("(p t) o -> p (t o)", t=PACK))
+        wa_raw.append(load_half("wa_raw1", wa, 1))
+        wb_raw = [load_half("wb_raw%d" % h, wb, h) for h in range(2)]
+        w1_raw = [load_half("w1_raw0", w1, 0)]
+        n2_t = load_list("n2_t", n2)
+        n1_t = load_list("n1_t", n1)
+        w1_raw.append(load_half("w1_raw1", w1, 1))
+        n3_t = load_list("n3_t", n3)
+        n4_t = load_list("n4_t", n4)
+
+        picked_bytes = []
+        for name, lst in (("a", offs_t), ("b", two_t)):
+            g = keep.tile([P, S], U8, name="picked_bytes_" + name, align_bytes=64)
+            nc.vector.tensor_copy(g[:], byte_table[:].indirect(lst[:]))
+            picked_bytes.append(g)
+        x_scale = []
+        for name, g in zip("ab", picked_bytes):
+            dealt = keep.tile([P, S], U8, name="x_scale_" + name, align_bytes=64)
+            nc.vector.tensor_copy(
+                dealt[:].rearrange("p (t s) -> p t s", t=PACK), g[:].rearrange("p (s t) -> p t s", t=PACK)
+            )
+            x_scale.append(dealt)
+
+        x_code = []
+        for name, lst in (("a", offs_t), ("b", two_t)):
+            g = keep.tile([P, S], U32, name="x_code_" + name, align_bytes=64)
+            nc.vector.tensor_copy(g[:].rearrange("p (t s) -> p s t", t=PACK), word_table[:].indirect(lst[:]))
+            x_code.append(g)
+
+        wa_mx = [mx_tiles("wa%d" % h, HALF) for h in range(2)]
+        wb_mx = [mx_tiles("wb%d" % h, HALF) for h in range(2)]
+        for h in range(2):
+            interleave(nc.scalar.copy, wa_mx[h], wa_raw[h])
+        for h in range(2):
+            quantize(wa_mx[h])
+
+        gain = keep.tile([P, PACK], F32, name="gain")
+        nc.gpsimd.tensor_scalar(gain[:], gt_raw[:], 0.75, 0.0, MULT, ADD)
+
+        def product(bank, lhs_codes, lhs_scales, t, mx):
+            cols = slice(t * P, (t + 1) * P)
+            nc.tensor.matmul_mx(
+                out=bank,
+                lhsT=lhs_codes[:, cols].bitcast(FP8X4),
+                lhsT_scale=lhs_scales[:, cols],
+                rhs=mx[1][:].bitcast(FP8X4),
+                rhs_scale=mx[2][:],
+                start=True,
+                stop=True,
+            )
+
+        y_bank = [psum.tile([P, H], F32, name="y_bank%d" % t, tag="lo%d" % t) for t in range(PACK)]
+        d_bank = [psum.tile([P, H], F32, name="d_bank%d" % t, tag="hi%d" % t) for t in range(PACK)]
+        for t in range(PACK):
+            for h in range(2):
+                product(y_bank[t][:, h * HALF : (h + 1) * HALF], x_code[0], x_scale[0], t, wa_mx[h])
+
+        y_win = [keep.tile([P, H + SPARE], F32, name="y_win%d" % t) for t in range(PACK)]
+        d_win = [keep.tile([P, H + SPARE], F32, name="d_win%d" % t) for t in range(PACK)]
+        h_win = [keep.tile([P, 2 * H], F32, name="h_win%d" % t) for t in range(PACK)]
+        tanh_win = [keep.tile([P, 2 * H], F32, name="tanh_win%d" % t) for t in range(PACK)]
+        first = keep.tile([P, PACK, H], F32, name="first")
+        second = keep.tile([P, PACK, H], F32, name="second")
+        w1_mx = mx_tiles("w1", N)
+
+        def deal_w1(copy, half):
+            places = slice(half * HALF // PACK, (half + 1) * HALF // PACK)
+            copy(
+                w1_mx[0][:].rearrange("p (t m j) -> p m j t", t=PACK, j=PACK)[:, places],
+                w1_raw[half][:].rearrange("p j (m t) -> p m j t", t=PACK),
+            )
+
+        interleave(nc.scalar.copy, wb_mx[0], wb_raw[0])
+        nc.vector.tensor_scalar(y_win[0][:, :H], y_bank[0][:], gain[:, 0:1], None, MULT)
+        quantize(wb_mx[0])
+        interleave(nc.vector.tensor_copy, wb_mx[1], wb_raw[1])
+        quantize(wb_mx[1])
+        deal_w1(nc.vector.tensor_copy, 0)
+        for h in range(2):
+            for t in range(PACK):
+                product(d_bank[t][:, h * HALF : (h + 1) * HALF], x_code[1], x_scale[1], t, wb_mx[h])
+
+        for t in range(1, PACK):
+            nc.scalar.activation(y_win[t][:, :H], y_bank[t][:], COPY, scale=gain[:, t : t + 1])
+        for t in range(PACK):
+            d_n2 = h_win[t][:, H:]
+            nc.scalar.copy(d_win[t][:, :H], d_bank[t][:])
+            nc.vector.tensor_tensor(second[:, t, :], y_win[t][:].indirect(n1_t[:]), d_win[t][:, :H], MULT)
+            nc.scalar.activation(d_n2, d_win[t][:].indirect(n2_t[:]), COPY)
+            nc.vector.tensor_tensor(first[:, t, :], y_win[t][:, :H], d_n2, MULT)
+        deal_w1(nc.scalar.copy, 1)
+
+        z_mx = [mx_tiles("z%d" % h, HALF) for h in range(2)]
+
+        def difference(h):
+            cols = slice(h * HALF, (h + 1) * HALF)
+            nc.vector.tensor_tensor(
+                z_mx[h][0][:].rearrange("p (c i t) -> p c t i", i=2, t=PACK),
+                first[:, :, cols].rearrange("p t (c i) -> p c t i", i=2),
+                second[:, :, cols].rearrange("p t (c i) -> p c t i", i=2),
+                SUB,
+            )
+
+        difference(0)
+        quantize(w1_mx)
+        quantize(z_mx[0])
+        difference(1)
+        quantize(z_mx[1])
+
+        h_bank = [
+            [psum.tile([P, HALF], F32, name="h_bank%d_%d" % (h, t), tag=("lo%d", "hi%d")[h] % t) for t in range(PACK)]
+            for h in range(2)
+        ]
+        for h in range(2):
+            for t in range(PACK):
+                product(h_bank[h][t][:], w1_mx[1], w1_mx[2], t, z_mx[h])
+
+        pair = [keep.tile([P, 2 * H], F32, name="pair%d" % t) for t in range(PACK)]
+        res = [keep.tile([P, H], F32, name="res%d" % t) for t in range(PACK)]
+        out_rows = out.rearrange("(p t) j -> p t j", t=PACK)
+
+        def h_copy(copy, h, t):
+            copy(h_win[t][:, h * HALF : (h + 1) * HALF], h_bank[h][t][:])
+
+        def tanh(h, t):
+            nc.scalar.activation(tanh_win[t][:, h * HALF : (h + 1) * HALF], h_bank[h][t][:], TANH)
+
+        def by_n3(t):
+            nc.scalar.activation(pair[t][:, H:], h_win[t][:].indirect(n3_t[:]), COPY)
+
+        def by_n4(t):
+            nc.vector.tensor_tensor(pair[t][:, :H], tanh_win[t][:].indirect(n4_t[:]), h_win[t][:, :H], MULT)
+
+        def finish(t):
+            nc.vector.tensor_tensor(res[t][:], pair[t][:, :H], pair[t][:, H:], MULT)
+            nc.sync.dma_start(out_rows[:, t, :], res[t][:])
+
+        for t in range(PACK):
+            tanh(0, t)
+            h_copy(nc.scalar.copy, 0, t)
+        for t in range(PACK):
+            h_copy(nc.vector.tensor_copy, 1, t)
+            tanh(1, t)
+        by_n4(0)
+        for t in range(PACK):
+            by_n3(t)
+            if t + 1 < PACK:
+                by_n4(t + 1)
+            finish(t)

@@ -22,6 +22,9 @@ P = 128
 PACK = 4
 HALF = 256
 SPARE = 16
+RUN = 4
+WB_RAW_AT = 8192
+QUARTER = 128
 
 
 def tile_picked_twtcrossbcube_none_p_kernel(
@@ -30,6 +33,7 @@ def tile_picked_twtcrossbcube_none_p_kernel(
     nc = tc.nc
     with ExitStack() as ctx:
         keep = ctx.enter_context(tc.tile_pool(name="keep", bufs=1))
+        shared = ctx.enter_context(tc.tile_pool(name="shared", bufs=1))
         psum = ctx.enter_context(tc.psum_pool(name="psum", bufs=1))
 
         def load_list(name, src):
@@ -37,14 +41,15 @@ def tile_picked_twtcrossbcube_none_p_kernel(
             nc.sync.dma_start(tile[:], src)
             return tile
 
-        def load_half(name, w, half):
-            raw = keep.tile([P, PACK, HALF], F32, name=name)
+        def load_half(name, w, half, pool=keep, offset=None):
+            raw = pool.tile([P, PACK, HALF], F32, name=name, align_bytes=64, offset=offset)
             cols = slice(half * HALF, (half + 1) * HALF)
             nc.sync.dma_start(raw[:], w.rearrange("(p j) c -> p j c", j=PACK)[:, :, cols])
             return raw
 
-        def mx_tiles(name, width):
-            grouped = keep.tile([P, width * PACK], BF16, name=name + "_bf", align_bytes=64)
+        def mx_tiles(name, width, grouped=None):
+            if grouped is None:
+                grouped = keep.tile([P, width * PACK], BF16, name=name + "_bf", align_bytes=64)
             codes = keep.tile([P, width], U32, name=name + "_codes", align_bytes=64)
             scales = keep.tile([P, width], U8, name=name + "_scales", align_bytes=64)
             return grouped, codes, scales
@@ -53,34 +58,39 @@ def tile_picked_twtcrossbcube_none_p_kernel(
             grouped, codes, scales = mx
             nc.vector.quantize_mx(out=codes[:].bitcast(FP8X4), scales=scales[:], in_=grouped[:])
 
-        def interleave(copy, mx, raw):
+        def interleave(copy, grouped, raw):
             copy(
-                mx[0][:].rearrange("p (c i j) -> p c j i", i=4, j=PACK),
+                grouped.rearrange("p (c i j) -> p c j i", i=4, j=PACK),
                 raw[:].rearrange("p j (c i) -> p c j i", i=4),
             )
 
         byte_table = keep.tile([P, T], U8, name="byte_table", align_bytes=64)
         nc.vector.memset(byte_table[:].bitcast(I32), 0)
         offs_t = load_list("offs_t", offs)
+        wa_raw = [load_half("wa_raw0", wa, 0)]
         for q in range(4):
             nc.sync.dma_start(
                 byte_table[32 * q : 32 * q + 4, :].bitcast(I32),
                 x_scales[0, 4 * q : 4 * q + 4, :].bitcast(I32),
             )
         two_t = load_list("two_t", two)
+        wa_raw.append(load_half("wa_raw1", wa, 1))
         word_table = keep.tile([P, T], U32, name="word_table", align_bytes=64)
         nc.sync.dma_start(
             word_table[:].bitcast(I32), x_words[0].rearrange("p c r -> p (c r)").bitcast(I32)
         )
-        wa_raw = [load_half("wa_raw0", wa, 0)]
+        wb_raw = [load_half("wb_raw0", wb, 0, shared, WB_RAW_AT), load_half("wb_raw1", wb, 1)]
         gt_raw = keep.tile([P, PACK], F32, name="gt_raw")
-        nc.sync.dma_start(gt_raw[:], gt.rearrange("(p t) o -> p (t o)", t=PACK))
-        wa_raw.append(load_half("wa_raw1", wa, 1))
-        wb_raw = [load_half("wb_raw%d" % h, wb, h) for h in range(2)]
-        w1_raw = [load_half("w1_raw0", w1, 0)]
+        gt_rows = gt.rearrange("(g t r) o -> r g (t o)", t=PACK, r=RUN)
+        with nc.allow_non_contiguous_dma(reason="one value a place"):
+            for r in range(RUN):
+                nc.sync.dma_start(gt_raw[r:P:RUN], gt_rows[r])
         n2_t = load_list("n2_t", n2)
         n1_t = load_list("n1_t", n1)
-        w1_raw.append(load_half("w1_raw1", w1, 1))
+        w1_raw = keep.tile([P, PACK, N], F32, name="w1_raw")
+        w1_rows = w1.rearrange("(g t r) m -> r g t m", t=PACK, r=RUN)
+        for r in range(RUN):
+            nc.sync.dma_start(w1_raw[r:P:RUN], w1_rows[r])
         n3_t = load_list("n3_t", n3)
         n4_t = load_list("n4_t", n4)
 
@@ -93,25 +103,23 @@ def tile_picked_twtcrossbcube_none_p_kernel(
         for name, g in zip("ab", picked_bytes):
             dealt = keep.tile([P, S], U8, name="x_scale_" + name, align_bytes=64)
             nc.vector.tensor_copy(
-                dealt[:].rearrange("p (t s) -> p t s", t=PACK), g[:].rearrange("p (s t) -> p t s", t=PACK)
+                dealt[:].bitcast(I32).rearrange("p (t g) -> p g t", t=PACK),
+                g[:].bitcast(I32).rearrange("p (g t) -> p g t", t=PACK),
             )
             x_scale.append(dealt)
+
+        wa_mx = mx_tiles("wa", H)
+        wb_mx = mx_tiles("wb", H, shared.tile([P, H * PACK], BF16, name="wb_bf", align_bytes=64, offset=0))
+        for h in range(2):
+            interleave(nc.scalar.copy, wa_mx[0][:, h * HALF * PACK : (h + 1) * HALF * PACK], wa_raw[h])
+        quantize(wa_mx)
 
         x_code = []
         for name, lst in (("a", offs_t), ("b", two_t)):
             g = keep.tile([P, S], U32, name="x_code_" + name, align_bytes=64)
-            nc.vector.tensor_copy(g[:].rearrange("p (t s) -> p s t", t=PACK), word_table[:].indirect(lst[:]))
+            nc.vector.tensor_copy(g[:].rearrange("p (t g r) -> p g t r", t=PACK, r=RUN), word_table[:].indirect(lst[:]))
             x_code.append(g)
 
-        wa_mx = [mx_tiles("wa%d" % h, HALF) for h in range(2)]
-        wb_mx = [mx_tiles("wb%d" % h, HALF) for h in range(2)]
-        for h in range(2):
-            interleave(nc.scalar.copy, wa_mx[h], wa_raw[h])
-        for h in range(2):
-            quantize(wa_mx[h])
-
-        gain = keep.tile([P, PACK], F32, name="gain")
-        nc.gpsimd.tensor_scalar(gain[:], gt_raw[:], 0.75, 0.0, MULT, ADD)
 
         def product(bank, lhs_codes, lhs_scales, t, mx):
             cols = slice(t * P, (t + 1) * P)
@@ -128,10 +136,8 @@ def tile_picked_twtcrossbcube_none_p_kernel(
         y_bank = [psum.tile([P, H], F32, name="y_bank%d" % t, tag="lo%d" % t) for t in range(PACK)]
         d_bank = [psum.tile([P, H], F32, name="d_bank%d" % t, tag="hi%d" % t) for t in range(PACK)]
         for t in range(PACK):
-            for h in range(2):
-                product(y_bank[t][:, h * HALF : (h + 1) * HALF], x_code[0], x_scale[0], t, wa_mx[h])
+            product(y_bank[t][:], x_code[0], x_scale[0], t, wa_mx)
 
-        y_win = [keep.tile([P, H + SPARE], F32, name="y_win%d" % t) for t in range(PACK)]
         d_win = [keep.tile([P, H + SPARE], F32, name="d_win%d" % t) for t in range(PACK)]
         h_win = [keep.tile([P, 2 * H], F32, name="h_win%d" % t) for t in range(PACK)]
         tanh_win = [keep.tile([P, 2 * H], F32, name="tanh_win%d" % t) for t in range(PACK)]
@@ -139,34 +145,54 @@ def tile_picked_twtcrossbcube_none_p_kernel(
         second = keep.tile([P, PACK, H], F32, name="second")
         w1_mx = mx_tiles("w1", N)
 
-        def deal_w1(copy, half):
-            places = slice(half * HALF // PACK, (half + 1) * HALF // PACK)
-            copy(
-                w1_mx[0][:].rearrange("p (t m j) -> p m j t", t=PACK, j=PACK)[:, places],
-                w1_raw[half][:].rearrange("p j (m t) -> p m j t", t=PACK),
-            )
+        interleave(nc.scalar.copy, wb_mx[0][:, : HALF * PACK], wb_raw[0])
+        interleave(nc.vector.tensor_copy, wb_mx[0][:, HALF * PACK :], wb_raw[1])
+        quantize(wb_mx)
+        places = (
+            (H + SPARE, WB_RAW_AT),
+            (H + SPARE, WB_RAW_AT + (H + SPARE) * 4),
+            (H, 0),
+            (H + SPARE, H * 4),
+        )
+        y_win = [
+            shared.tile([P, width], F32, name="y_win%d" % t, align_bytes=64, offset=offset)
+            for t, (width, offset) in enumerate(places)
+        ]
+        for t in (2, 3):
+            nc.vector.tensor_copy(y_win[t][:, :H], y_bank[t][:])
+        for t in range(PACK):
+            product(d_bank[t][:], x_code[1], x_scale[1], t, wb_mx)
 
-        interleave(nc.scalar.copy, wb_mx[0], wb_raw[0])
-        nc.vector.tensor_scalar(y_win[0][:, :H], y_bank[0][:], gain[:, 0:1], None, MULT)
-        quantize(wb_mx[0])
-        interleave(nc.vector.tensor_copy, wb_mx[1], wb_raw[1])
-        quantize(wb_mx[1])
-        deal_w1(nc.vector.tensor_copy, 0)
-        for h in range(2):
-            for t in range(PACK):
-                product(d_bank[t][:, h * HALF : (h + 1) * HALF], x_code[1], x_scale[1], t, wb_mx[h])
-
-        for t in range(1, PACK):
-            nc.scalar.activation(y_win[t][:, :H], y_bank[t][:], COPY, scale=gain[:, t : t + 1])
+        for t in range(2):
+            nc.scalar.copy(y_win[t][:, :H], y_bank[t][:])
+        gain = keep.tile([P, PACK], F32, name="gain")
+        nc.gpsimd.tensor_scalar(gain[:], gt_raw[:], 0.75, 0.0, MULT, ADD)
+        halves = [slice(h * HALF, (h + 1) * HALF) for h in range(2)]
         for t in range(PACK):
             d_n2 = h_win[t][:, H:]
-            nc.scalar.copy(d_win[t][:, :H], d_bank[t][:])
-            nc.vector.tensor_tensor(second[:, t, :], y_win[t][:].indirect(n1_t[:]), d_win[t][:, :H], MULT)
+            nc.scalar.activation(d_win[t][:, :H], d_bank[t][:], COPY, scale=gain[:, t : t + 1])
+            if t == 2:
+                for h in range(2):
+                    nc.vector.tensor_tensor(
+                        second[:, t, halves[h]],
+                        y_win[t][:].indirect(n1_t[:, 16 * h : 16 * (h + 1)]),
+                        d_win[t][:, halves[h]],
+                        MULT,
+                    )
+            else:
+                nc.vector.tensor_tensor(second[:, t, :], y_win[t][:].indirect(n1_t[:]), d_win[t][:, :H], MULT)
             nc.scalar.activation(d_n2, d_win[t][:].indirect(n2_t[:]), COPY)
-            nc.vector.tensor_tensor(first[:, t, :], y_win[t][:, :H], d_n2, MULT)
-        deal_w1(nc.scalar.copy, 1)
+            for cols in halves if t == PACK - 1 else [slice(0, H)]:
+                nc.vector.tensor_tensor(first[:, t, cols], y_win[t][:, cols], d_n2[:, cols], MULT)
+        nc.scalar.copy(
+            w1_mx[0][:].rearrange("p (t m j) -> p m j t", t=PACK, j=PACK),
+            w1_raw[:].rearrange("p j (m t) -> p m j t", t=PACK),
+        )
 
-        z_mx = [mx_tiles("z%d" % h, HALF) for h in range(2)]
+        z_mx = [
+            mx_tiles("z0", HALF),
+            mx_tiles("z1", HALF, keep.tile([P, HALF * PACK], BF16, name="z1_bf", tag="w1_bf", align_bytes=64)),
+        ]
 
         def difference(h):
             cols = slice(h * HALF, (h + 1) * HALF)
@@ -178,8 +204,8 @@ def tile_picked_twtcrossbcube_none_p_kernel(
             )
 
         difference(0)
-        quantize(w1_mx)
         quantize(z_mx[0])
+        quantize(w1_mx)
         difference(1)
         quantize(z_mx[1])
 
@@ -208,18 +234,24 @@ def tile_picked_twtcrossbcube_none_p_kernel(
             nc.vector.tensor_tensor(pair[t][:, :H], tanh_win[t][:].indirect(n4_t[:]), h_win[t][:, :H], MULT)
 
         def finish(t):
-            nc.vector.tensor_tensor(res[t][:], pair[t][:, :H], pair[t][:, H:], MULT)
-            nc.sync.dma_start(out_rows[:, t, :], res[t][:])
+            for cols in halves if t == PACK - 1 else [slice(0, H)]:
+                nc.vector.tensor_tensor(res[t][:, cols], pair[t][:, cols], pair[t][:, H:][:, cols], MULT)
+                nc.sync.dma_start(out_rows[:, t, cols], res[t][:, cols])
 
         for t in range(PACK):
             tanh(0, t)
-            h_copy(nc.scalar.copy, 0, t)
-        for t in range(PACK):
-            h_copy(nc.vector.tensor_copy, 1, t)
-            tanh(1, t)
+            h_copy(nc.vector.tensor_copy, 0, t)
+        tanh(1, 0)
+        h_copy(nc.scalar.copy, 1, 0)
+        h_copy(nc.vector.tensor_copy, 1, 1)
+        tanh(1, 1)
         by_n4(0)
-        for t in range(PACK):
-            by_n3(t)
+        by_n3(0)
+        for t in range(1, PACK):
             if t + 1 < PACK:
-                by_n4(t + 1)
-            finish(t)
+                tanh(1, t + 1)
+                h_copy(nc.scalar.copy, 1, t + 1)
+            by_n4(t)
+            finish(t - 1)
+            by_n3(t)
+        finish(PACK - 1)

from contextlib import ExitStack

import concourse.mybir as mybir

K, T, S, N, H = 512, 2048, 512, 512, 512
FLOPS = 2 * K * S * H * 2 + 2 * S * N * H

F32 = mybir.dt.float32
BF16 = mybir.dt.bfloat16
I32 = mybir.dt.int32
U32 = mybir.dt.uint32
U16 = mybir.dt.uint16
U8 = mybir.dt.uint8
FP8X4 = mybir.dt.float8_e4m3fn_x4
MULT = mybir.AluOpType.mult
ADD = mybir.AluOpType.add
SUB = mybir.AluOpType.subtract
COPY = mybir.ActivationFunctionType.Copy
TANH = mybir.ActivationFunctionType.Tanh

P = 128
PACK = 4
HALF = 256
SPARE = 16
RUN = 4
WB_RAW_AT = 8192
QUARTER = 128


def tile_picked_twtcrossbcube_none_p_kernel(
    tc, x_words, x_scales, wa, wb, gt, w1, offs, two, n1, n2, n3, n4, out
):
    nc = tc.nc
    with ExitStack() as ctx:
        keep = ctx.enter_context(tc.tile_pool(name="keep", bufs=1))
        shared = ctx.enter_context(tc.tile_pool(name="shared", bufs=1))
        psum = ctx.enter_context(tc.psum_pool(name="psum", bufs=1))

        def load_list(name, src):
            tile = keep.tile([P, S // 16], U16, name=name)
            nc.sync.dma_start(tile[:], src)
            return tile

        def load_half(name, w, half, pool=keep, offset=None):
            raw = pool.tile([P, PACK, HALF], F32, name=name, align_bytes=64, offset=offset)
            cols = slice(half * HALF, (half + 1) * HALF)
            nc.sync.dma_start(raw[:], w.rearrange("(p j) c -> p j c", j=PACK)[:, :, cols])
            return raw

        def mx_tiles(name, width, grouped=None):
            if grouped is None:
                grouped = keep.tile([P, width * PACK], BF16, name=name + "_bf", align_bytes=64)
            codes = keep.tile([P, width], U32, name=name + "_codes", align_bytes=64)
            scales = keep.tile([P, width], U8, name=name + "_scales", align_bytes=64)
            return grouped, codes, scales

        def quantize(mx):
            grouped, codes, scales = mx
            nc.vector.quantize_mx(out=codes[:].bitcast(FP8X4), scales=scales[:], in_=grouped[:])

        def interleave(copy, grouped, raw):
            copy(
                grouped.rearrange("p (c i j) -> p c j i", i=4, j=PACK),
                raw[:].rearrange("p j (c i) -> p c j i", i=4),
            )

        byte_table = keep.tile([P, T], U8, name="byte_table", align_bytes=64)
        nc.vector.memset(byte_table[:].bitcast(I32), 0)
        offs_t = load_list("offs_t", offs)
        wa_raw = [load_half("wa_raw0", wa, 0)]
        for q in range(4):
            nc.sync.dma_start(
                byte_table[32 * q : 32 * q + 4, :].bitcast(I32),
                x_scales[0, 4 * q : 4 * q + 4, :].bitcast(I32),
            )
        two_t = load_list("two_t", two)
        wa_raw.append(load_half("wa_raw1", wa, 1))
        word_table = keep.tile([P, T], U32, name="word_table", align_bytes=64)
        nc.sync.dma_start(
            word_table[:].bitcast(I32), x_words[0].rearrange("p c r -> p (c r)").bitcast(I32)
        )
        wb_raw = [load_half("wb_raw0", wb, 0, shared, WB_RAW_AT), load_half("wb_raw1", wb, 1)]
        gt_raw = keep.tile([P, PACK], F32, name="gt_raw")
        gt_rows = gt.rearrange("(g t r) o -> r g (t o)", t=PACK, r=RUN)
        with nc.allow_non_contiguous_dma(reason="one value a place"):
            for r in range(RUN):
                nc.sync.dma_start(gt_raw[r:P:RUN], gt_rows[r])
        n2_t = load_list("n2_t", n2)
        n1_t = load_list("n1_t", n1)
        w1_raw = keep.tile([P, PACK, N], F32, name="w1_raw")
        w1_rows = w1.rearrange("(g t r) m -> r g t m", t=PACK, r=RUN)
        for r in range(RUN):
            nc.sync.dma_start(w1_raw[r:P:RUN], w1_rows[r])
        n3_t = load_list("n3_t", n3)
        n4_t = load_list("n4_t", n4)

        picked_bytes = []
        for name, lst in (("a", offs_t), ("b", two_t)):
            g = keep.tile([P, S], U8, name="picked_bytes_" + name, align_bytes=64)
            nc.vector.tensor_copy(g[:], byte_table[:].indirect(lst[:]))
            picked_bytes.append(g)
        x_scale = []
        for name, g in zip("ab", picked_bytes):
            dealt = keep.tile([P, S], U8, name="x_scale_" + name, align_bytes=64)
            nc.vector.tensor_copy(
                dealt[:].bitcast(I32).rearrange("p (t g) -> p g t", t=PACK),
                g[:].bitcast(I32).rearrange("p (g t) -> p g t", t=PACK),
            )
            x_scale.append(dealt)

        wa_mx = mx_tiles("wa", H)
        wb_mx = mx_tiles("wb", H, shared.tile([P, H * PACK], BF16, name="wb_bf", align_bytes=64, offset=0))
        for h in range(2):
            interleave(nc.scalar.copy, wa_mx[0][:, h * HALF * PACK : (h + 1) * HALF * PACK], wa_raw[h])
        quantize(wa_mx)

        x_code = []
        for name, lst in (("a", offs_t), ("b", two_t)):
            g = keep.tile([P, S], U32, name="x_code_" + name, align_bytes=64)
            nc.vector.tensor_copy(g[:].rearrange("p (t g r) -> p g t r", t=PACK, r=RUN), word_table[:].indirect(lst[:]))
            x_code.append(g)


        def product(bank, lhs_codes, lhs_scales, t, mx):
            cols = slice(t * P, (t + 1) * P)
            nc.tensor.matmul_mx(
                out=bank,
                lhsT=lhs_codes[:, cols].bitcast(FP8X4),
                lhsT_scale=lhs_scales[:, cols],
                rhs=mx[1][:].bitcast(FP8X4),
                rhs_scale=mx[2][:],
                start=True,
                stop=True,
            )

        y_bank = [psum.tile([P, H], F32, name="y_bank%d" % t, tag="lo%d" % t) for t in range(PACK)]
        d_bank = [psum.tile([P, H], F32, name="d_bank%d" % t, tag="hi%d" % t) for t in range(PACK)]
        for t in range(PACK):
            product(y_bank[t][:], x_code[0], x_scale[0], t, wa_mx)

        d_win = [keep.tile([P, H + SPARE], F32, name="d_win%d" % t) for t in range(PACK)]
        h_win = [keep.tile([P, 2 * H], F32, name="h_win%d" % t) for t in range(PACK)]
        tanh_win = [keep.tile([P, 2 * H], F32, name="tanh_win%d" % t) for t in range(PACK)]
        first = keep.tile([P, PACK, H], F32, name="first")
        second = keep.tile([P, PACK, H], F32, name="second")
        w1_mx = mx_tiles("w1", N)

        interleave(nc.scalar.copy, wb_mx[0][:, : HALF * PACK], wb_raw[0])
        interleave(nc.vector.tensor_copy, wb_mx[0][:, HALF * PACK :], wb_raw[1])
        quantize(wb_mx)
        places = (
            (H + SPARE, WB_RAW_AT),
            (H + SPARE, WB_RAW_AT + (H + SPARE) * 4),
            (H, 0),
            (H + SPARE, H * 4),
        )
        y_win = [
            shared.tile([P, width], F32, name="y_win%d" % t, align_bytes=64, offset=offset)
            for t, (width, offset) in enumerate(places)
        ]
        for t in (2, 3):
            nc.vector.tensor_copy(y_win[t][:, :H], y_bank[t][:])
        for t in range(PACK):
            product(d_bank[t][:], x_code[1], x_scale[1], t, wb_mx)

        for t in range(2):
            nc.scalar.copy(y_win[t][:, :H], y_bank[t][:])
        gain = keep.tile([P, PACK], F32, name="gain")
        nc.gpsimd.tensor_scalar(gain[:], gt_raw[:], 0.75, 0.0, MULT, ADD)
        halves = [slice(h * HALF, (h + 1) * HALF) for h in range(2)]
        for t in range(PACK):
            d_n2 = h_win[t][:, H:]
            nc.scalar.activation(d_win[t][:, :H], d_bank[t][:], COPY, scale=gain[:, t : t + 1])
            if t == 2:
                for h in range(2):
                    nc.vector.tensor_tensor(
                        second[:, t, halves[h]],
                        y_win[t][:].indirect(n1_t[:, 16 * h : 16 * (h + 1)]),
                        d_win[t][:, halves[h]],
                        MULT,
                    )
            else:
                nc.vector.tensor_tensor(second[:, t, :], y_win[t][:].indirect(n1_t[:]), d_win[t][:, :H], MULT)
            nc.scalar.activation(d_n2, d_win[t][:].indirect(n2_t[:]), COPY)
            for cols in halves if t == PACK - 1 else [slice(0, H)]:
                nc.vector.tensor_tensor(first[:, t, cols], y_win[t][:, cols], d_n2[:, cols], MULT)
        nc.scalar.copy(
            w1_mx[0][:].rearrange("p (t m j) -> p m j t", t=PACK, j=PACK),
            w1_raw[:].rearrange("p j (m t) -> p m j t", t=PACK),
        )

        z_mx = [
            mx_tiles("z0", HALF),
            mx_tiles("z1", HALF, keep.tile([P, HALF * PACK], BF16, name="z1_bf", tag="w1_bf", align_bytes=64)),
        ]

        def difference(h):
            cols = slice(h * HALF, (h + 1) * HALF)
            nc.vector.tensor_tensor(
                z_mx[h][0][:].rearrange("p (c i t) -> p c t i", i=2, t=PACK),
                first[:, :, cols].rearrange("p t (c i) -> p c t i", i=2),
                second[:, :, cols].rearrange("p t (c i) -> p c t i", i=2),
                SUB,
            )

        difference(0)
        quantize(z_mx[0])
        quantize(w1_mx)
        difference(1)
        quantize(z_mx[1])

        h_bank = [
            [psum.tile([P, HALF], F32, name="h_bank%d_%d" % (h, t), tag=("lo%d", "hi%d")[h] % t) for t in range(PACK)]
            for h in range(2)
        ]
        for h in range(2):
            for t in range(PACK):
                product(h_bank[h][t][:], w1_mx[1], w1_mx[2], t, z_mx[h])

        pair = [keep.tile([P, 2 * H], F32, name="pair%d" % t) for t in range(PACK)]
        res = [keep.tile([P, H], F32, name="res%d" % t) for t in range(PACK)]
        out_rows = out.rearrange("(p t) j -> p t j", t=PACK)

        def h_copy(copy, h, t):
            copy(h_win[t][:, h * HALF : (h + 1) * HALF], h_bank[h][t][:])

        def tanh(h, t):
            nc.scalar.activation(tanh_win[t][:, h * HALF : (h + 1) * HALF], h_bank[h][t][:], TANH)

        def by_n3(t):
            nc.scalar.activation(pair[t][:, H:], h_win[t][:].indirect(n3_t[:]), COPY)

        def by_n4(t):
            nc.vector.tensor_tensor(pair[t][:, :H], tanh_win[t][:].indirect(n4_t[:]), h_win[t][:, :H], MULT)

        def finish(t):
            for cols in halves if t == PACK - 1 else [slice(0, H)]:
                nc.vector.tensor_tensor(res[t][:, cols], pair[t][:, cols], pair[t][:, H:][:, cols], MULT)
                nc.sync.dma_start(out_rows[:, t, cols], res[t][:, cols])

        for t in range(PACK):
            tanh(0, t)
            h_copy(nc.vector.tensor_copy, 0, t)
        tanh(1, 0)
        h_copy(nc.scalar.copy, 1, 0)
        h_copy(nc.vector.tensor_copy, 1, 1)
        tanh(1, 1)
        by_n4(0)
        by_n3(0)
        for t in range(1, PACK):
            if t + 1 < PACK:
                tanh(1, t + 1)
                h_copy(nc.scalar.copy, 1, t + 1)
            by_n4(t)
            finish(t - 1)
            by_n3(t)
        finish(PACK - 1)
